import numpy as np
import ml_dtypes

BF16 = ml_dtypes.bfloat16


def bf(x):
    return np.asarray(x, np.float32).astype(BF16)


def f32(x):
    return np.asarray(x, np.float32)


def f64(x):
    return np.asarray(x).astype(np.float64)


def striped(idx):
    return np.tile(idx.reshape(-1, 16).T, (8, 1))


S, A, K, M, N, E, Q = 512, 256, 128, 128, 512, 4, 128


def setup_inputs():
    return {"x": bf(np.random.standard_normal((A, S))), "wd": bf(np.random.standard_normal((A, M)) / np.sqrt(A)), "y": bf(np.random.standard_normal((K, N))), "w": bf(np.random.standard_normal((E, K, M)) / np.sqrt(K)), "b": f32(0.5 * np.random.standard_normal((M, 1))), "offs": striped(np.random.permutation(S))}


def reference(x, wd, y, w, b, offs):
    idx = offs[:16].T.reshape(-1)
    z = f64(wd).T @ f64(x)
    for e in range(E):
        z[:, idx[e * Q : (e + 1) * Q]] += f64(w)[e].T @ f64(y)[:, e * Q : (e + 1) * Q]
    return np.tanh(z + f64(b))

@@ -1,0 +1,50 @@
+import concourse.mybir as mybir
+
+D, M, S = 256, 128, 512
+E, K, N = 4, 128, 512
+Q = N // E
+P = 128
+A = D // P
+
+FLOPS = 2 * M * D * S + 2 * M * K * N
+
+BF16, F32, U16 = mybir.dt.bfloat16, mybir.dt.float32, mybir.dt.uint16
+TANH = mybir.ActivationFunctionType.Tanh
+
+
+def tile_rows_fillproj_tanh_kernel(tc, x, wd, y, w, b, offs, out):
+    nc = tc.nc
+    with (
+        tc.tile_pool(name="held", bufs=1) as held,
+        tc.psum_pool(name="psum", bufs=1) as psum,
+    ):
+        wd_tile = held.tile([P, A, M], BF16)
+        nc.sync.dma_start(wd_tile[:], wd.rearrange("(p a) m -> p a m", a=A))
+        x_tile = held.tile([P, A, S], BF16)
+        nc.sync.dma_start(x_tile[:], x.rearrange("(p a) s -> p a s", a=A))
+        offsets = held.tile([P, N // 16], U16)
+        nc.sync.dma_start(offsets[:], offs)
+        y_tile = held.tile([P, N], BF16)
+        nc.sync.dma_start(y_tile[:], y)
+        w_tile = held.tile([P, E, M], BF16)
+        nc.sync.dma_start(w_tile[:], w.rearrange("e k m -> k e m"))
+        bias = held.tile([P, 1], F32)
+        nc.sync.dma_start(bias[:], b)
+
+        window = psum.tile([M, S], F32)
+        for a in range(A):
+            nc.tensor.matmul(window[:], wd_tile[:, a, :], x_tile[:, a, :], start=(a == 0), stop=False)
+
+        for e in range(E):
+            piece = offsets[:, e * Q // 16 : (e + 1) * Q // 16]
+            nc.tensor.matmul(
+                window[:].indirect(piece),
+                w_tile[:, e, :],
+                y_tile[:, e * Q : (e + 1) * Q],
+                start=False,
+                stop=(e == E - 1),
+            )
+
+        result = held.tile([M, S], F32)
+        nc.scalar.activation(result[:], window[:], TANH, bias=bias[:])
+        nc.sync.dma_start(out, result[:])

@@ -5,6 +5,7 @@ E, K, N = 4, 128, 512
 Q = N // E
 P = 128
 A = D // P
+WARM_MATMULS = 4
 
 FLOPS = 2 * M * D * S + 2 * M * K * N
 
@@ -30,6 +31,14 @@ def tile_rows_fillproj_tanh_kernel(tc, x, wd, y, w, b, offs, out):
         nc.sync.dma_start(w_tile[:], w.rearrange("e k m -> k e m"))
         bias = held.tile([P, 1], F32)
         nc.sync.dma_start(bias[:], b)
+
+        zeros = held.tile([P, S], BF16)
+        nc.vector.memset(zeros[:], 0.0)
+        warm_bank = psum.tile([P, S], F32)
+        for i in range(WARM_MATMULS):
+            nc.tensor.matmul(warm_bank[:], zeros[:, :P], zeros[:], start=True, stop=True)
+        early_tanh = held.tile([P, 1], F32)
+        nc.scalar.activation(early_tanh[:], zeros[:, :1], TANH)
 
         window = psum.tile([M, S], F32)
         for a in range(A):

@@ -5,7 +5,7 @@ E, K, N = 4, 128, 512
 Q = N // E
 P = 128
 A = D // P
-WARM_MATMULS = 4
+WARM_COLUMNS, WARM_MATMULS = 256, 7
 
 FLOPS = 2 * M * D * S + 2 * M * K * N
 
@@ -20,7 +20,7 @@ def tile_rows_fillproj_tanh_kernel(tc, x, wd, y, w, b, offs, out):
         tc.psum_pool(name="psum", bufs=1) as psum,
     ):
         wd_tile = held.tile([P, A, M], BF16)
-        nc.sync.dma_start(wd_tile[:], wd.rearrange("(p a) m -> p a m", a=A))
+        nc.scalar.dma_start(wd_tile[:], wd.rearrange("(p a) m -> p a m", a=A))
         x_tile = held.tile([P, A, S], BF16)
         nc.sync.dma_start(x_tile[:], x.rearrange("(p a) s -> p a s", a=A))
         offsets = held.tile([P, N // 16], U16)
@@ -28,13 +28,13 @@ def tile_rows_fillproj_tanh_kernel(tc, x, wd, y, w, b, offs, out):
         y_tile = held.tile([P, N], BF16)
         nc.sync.dma_start(y_tile[:], y)
         w_tile = held.tile([P, E, M], BF16)
-        nc.sync.dma_start(w_tile[:], w.rearrange("e k m -> k e m"))
+        nc.scalar.dma_start(w_tile[:], w.rearrange("e k m -> k e m"))
         bias = held.tile([P, 1], F32)
-        nc.sync.dma_start(bias[:], b)
+        nc.scalar.dma_start(bias[:], b)
 
-        zeros = held.tile([P, S], BF16)
+        zeros = held.tile([P, WARM_COLUMNS], BF16)
         nc.vector.memset(zeros[:], 0.0)
-        warm_bank = psum.tile([P, S], F32)
+        warm_bank = psum.tile([P, WARM_COLUMNS], F32)
         for i in range(WARM_MATMULS):
             nc.tensor.matmul(warm_bank[:], zeros[:, :P], zeros[:], start=True, stop=True)
         early_tanh = held.tile([P, 1], F32)
@@ -55,5 +55,8 @@ def tile_rows_fillproj_tanh_kernel(tc, x, wd, y, w, b, offs, out):
             )
 
         result = held.tile([M, S], F32)
-        nc.scalar.activation(result[:], window[:], TANH, bias=bias[:])
-        nc.sync.dma_start(out, result[:])
+        half = S // 2
+        for h in range(2):
+            columns = slice(h * half, (h + 1) * half)
+            nc.scalar.activation(result[:, columns], window[:, columns], TANH, bias=bias[:])
+            nc.sync.dma_start(out[:, columns], result[:, columns])

@@ -20,7 +20,7 @@ def tile_rows_fillproj_tanh_kernel(tc, x, wd, y, w, b, offs, out):
         tc.psum_pool(name="psum", bufs=1) as psum,
     ):
         wd_tile = held.tile([P, A, M], BF16)
-        nc.scalar.dma_start(wd_tile[:], wd.rearrange("(p a) m -> p a m", a=A))
+        nc.sync.dma_start(wd_tile[:], wd.rearrange("(p a) m -> p a m", a=A))
         x_tile = held.tile([P, A, S], BF16)
         nc.sync.dma_start(x_tile[:], x.rearrange("(p a) s -> p a s", a=A))
         offsets = held.tile([P, N // 16], U16)
@@ -28,9 +28,9 @@ def tile_rows_fillproj_tanh_kernel(tc, x, wd, y, w, b, offs, out):
         y_tile = held.tile([P, N], BF16)
         nc.sync.dma_start(y_tile[:], y)
         w_tile = held.tile([P, E, M], BF16)
-        nc.scalar.dma_start(w_tile[:], w.rearrange("e k m -> k e m"))
+        nc.sync.dma_start(w_tile[:], w.rearrange("e k m -> k e m"))
         bias = held.tile([P, 1], F32)
-        nc.scalar.dma_start(bias[:], b)
+        nc.sync.dma_start(bias[:], b)
 
         zeros = held.tile([P, WARM_COLUMNS], BF16)
         nc.vector.memset(zeros[:], 0.0)

import concourse.mybir as mybir

D, M, S = 256, 128, 512
E, K, N = 4, 128, 512
Q = N // E
P = 128
A = D // P
WARM_COLUMNS, WARM_MATMULS = 256, 7

FLOPS = 2 * M * D * S + 2 * M * K * N

BF16, F32, U16 = mybir.dt.bfloat16, mybir.dt.float32, mybir.dt.uint16
TANH = mybir.ActivationFunctionType.Tanh


def tile_rows_fillproj_tanh_kernel(tc, x, wd, y, w, b, offs, out):
    nc = tc.nc
    with (
        tc.tile_pool(name="held", bufs=1) as held,
        tc.psum_pool(name="psum", bufs=1) as psum,
    ):
        wd_tile = held.tile([P, A, M], BF16)
        nc.sync.dma_start(wd_tile[:], wd.rearrange("(p a) m -> p a m", a=A))
        x_tile = held.tile([P, A, S], BF16)
        nc.sync.dma_start(x_tile[:], x.rearrange("(p a) s -> p a s", a=A))
        offsets = held.tile([P, N // 16], U16)
        nc.sync.dma_start(offsets[:], offs)
        y_tile = held.tile([P, N], BF16)
        nc.sync.dma_start(y_tile[:], y)
        w_tile = held.tile([P, E, M], BF16)
        nc.sync.dma_start(w_tile[:], w.rearrange("e k m -> k e m"))
        bias = held.tile([P, 1], F32)
        nc.sync.dma_start(bias[:], b)

        zeros = held.tile([P, WARM_COLUMNS], BF16)
        nc.vector.memset(zeros[:], 0.0)
        warm_bank = psum.tile([P, WARM_COLUMNS], F32)
        for i in range(WARM_MATMULS):
            nc.tensor.matmul(warm_bank[:], zeros[:, :P], zeros[:], start=True, stop=True)
        early_tanh = held.tile([P, 1], F32)
        nc.scalar.activation(early_tanh[:], zeros[:, :1], TANH)

        window = psum.tile([M, S], F32)
        for a in range(A):
            nc.tensor.matmul(window[:], wd_tile[:, a, :], x_tile[:, a, :], start=(a == 0), stop=False)

        for e in range(E):
            piece = offsets[:, e * Q // 16 : (e + 1) * Q // 16]
            nc.tensor.matmul(
                window[:].indirect(piece),
                w_tile[:, e, :],
                y_tile[:, e * Q : (e + 1) * Q],
                start=False,
                stop=(e == E - 1),
            )

        result = held.tile([M, S], F32)
        half = S // 2
        for h in range(2):
            columns = slice(h * half, (h + 1) * half)
            nc.scalar.activation(result[:, columns], window[:, columns], TANH, bias=bias[:])
            nc.sync.dma_start(out[:, columns], result[:, columns])
